import numpy as np
import ml_dtypes


def mxq(x, axis, fmt="e4m3"):
    dtype, down = {"e4m3": (ml_dtypes.float8_e4m3fn, 7), "e5m2": (ml_dtypes.float8_e5m2, 14)}[fmt]
    v = np.moveaxis(np.asarray(x, np.float32).astype(ml_dtypes.bfloat16).astype(np.float64), axis, -1)
    blocks = v.reshape(v.shape[:-1] + (-1, 32))
    amax = np.abs(blocks).max(-1, keepdims=True)
    byte = np.maximum(np.where(amax > 0, np.frexp(amax)[1] - 1 + 127, 0) - down, 1)
    scale = np.exp2(byte - 127.0)
    codes = (blocks / scale).astype(np.float32).astype(dtype).astype(np.float64)
    return np.moveaxis((codes * scale).reshape(v.shape), -1, axis)


WIDE = False


def mx_kscale(k):
    if not WIDE:
        return np.ones(k)
    levels = np.array([10, -10, 5, -5, 0])
    if k % 512:
        return np.exp2(np.random.permutation(np.resize(levels, k // 32))).repeat(32)
    a = np.empty((k // 512, 16))
    for p in range(k // 512):
        a[p, :8] = np.random.permutation(np.resize(levels, 8))
        for g in range(8):
            far = levels[np.abs(levels - a[p, g]) >= 10]
            a[p, g + 8] = far[np.random.randint(len(far))]
    return np.exp2(a.ravel()).repeat(32)


def f64(x):
    return np.asarray(x).astype(np.float64)


def striped(idx):
    return np.tile(idx.reshape(-1, 16).T, (8, 1)).astype(np.uint16)


def unstriped(offs):
    return offs[:16].T.reshape(-1).astype(np.int64)


def pack_weight(w):
    k, n = w.shape
    w = f64(np.asarray(w, np.float32).astype(ml_dtypes.bfloat16)).reshape(k // 32, 32, n)
    amax = np.abs(w).max(1)
    byte = np.clip(np.where(amax > 0, np.frexp(amax)[1] - 1 + 127 - 7, 1), 1, 254)
    scaled = (w * np.exp2(127.0 - byte)[:, None, :]).reshape(k, n).astype(np.float32)
    words = np.ascontiguousarray(scaled.reshape(k // 512, 128, 4, n).transpose(0, 1, 3, 2)).astype(ml_dtypes.float8_e4m3fn).view(np.uint8)
    return words, np.ascontiguousarray(byte.astype(np.uint8).reshape(k // 512, 16, n))


def unpack_weight(words, scales):
    g, p, n, _ = words.shape
    vals = np.ascontiguousarray(words).view(ml_dtypes.float8_e4m3fn).astype(np.float64) * np.repeat(np.exp2(scales.astype(np.float64) - 127.0), 8, axis=1)[..., None]
    return vals.transpose(0, 1, 3, 2).reshape(g * 512, n)


def relu(v):
    return np.maximum(v, 0.0)


K, T, S, D, H, N, V, U = 1024, 2048, 512, 4, 512, 256, 128, 512
P = 2 ** 7


def setup_inputs():
    n = np.random.standard_normal
    s = mx_kscale(K)[:, None]
    u = mx_kscale(H)
    packed_xT = pack_weight(n((K, T)) * s)
    return {
        "x_words": packed_xT[0],
        "x_scales": packed_xT[1],
        "w1": (n((K, H)) / np.sqrt(K) / s * u).astype(np.float32),
        "w2": (n((H, N)) / np.sqrt(H) / u[:, None]).astype(np.float32),
        "accel": (n((N, S))).astype(np.float32),
        "dt": (np.tile(np.random.uniform(0.2, 0.6, S), (P, 1))).astype(np.float32),
        "lev": (np.tile(np.random.uniform(0.1, 1.0, S), (P, 1))).astype(np.float32),
        "vel": (n((N, U))).astype(np.float32),
        "posi": (n((N, U))).astype(np.float32),
        "tt": (np.tile(np.random.uniform(0.8, 2.0, V), (P, 1))).astype(np.float32),
        "wv": (np.random.uniform(0.3, 1.0, (N, 1))).astype(np.float32),
        "wpp": (np.random.uniform(0.3, 1.0, (N, 1))).astype(np.float32),
        "offs": striped(np.random.permutation(T)[:S]),
        "from1": striped(np.random.randint(0, U, V)),
        "to1": striped(np.random.randint(0, U, V)),
    }


def reference(x_words, x_scales, w1, w2, accel, dt, lev, vel, posi, tt, wv, wpp, offs, from1, to1):
    xq = unpack_weight(x_words, x_scales)[:, unstriped(offs)]
    h = relu(mxq(f64(w1), 0, "e4m3").T @ xq)
    a0 = f64(accel) + 0.3 * ((mxq(f64(w2), 0, "e4m3").T @ mxq(h, 0, "e4m3")))
    av = a0 * f64(dt)[:1]
    dv = av.reshape(len(av), -1, D).sum(axis=2)
    rv = f64(vel)[:, unstriped(to1)] - f64(vel)[:, unstriped(from1)] - dv
    ap = a0 * f64(lev)[:1]
    dp = ap.reshape(len(ap), -1, D).sum(axis=2)
    rp = f64(posi)[:, unstriped(to1)] - f64(posi)[:, unstriped(from1)] - (f64(vel)[:, unstriped(from1)] * f64(tt)[:1]) - dp
    return f64(wv) * ((rv) ** 2) + f64(wpp) * ((rp) ** 2)

@@ -1,0 +1,246 @@
+from contextlib import ExitStack
+
+import concourse.mybir as mybir
+from concourse.masks import make_identity
+
+F32 = mybir.dt.float32
+BF16 = mybir.dt.bfloat16
+I32 = mybir.dt.int32
+U32 = mybir.dt.uint32
+U16 = mybir.dt.uint16
+U8 = mybir.dt.uint8
+FP8X4 = mybir.dt.float8_e4m3fn_x4
+ALU = mybir.AluOpType
+ACT = mybir.ActivationFunctionType
+
+K, T, S, D, H, N, V, U = 1024, 2048, 512, 4, 512, 256, 128, 512
+P = 128
+PACK = 4
+PASSES = K // (P * PACK)
+CHUNK = 128
+CHUNKS = S // CHUNK
+ROW_TILES = N // P
+GAIN = 0.3
+W1_VECTOR_SHARE = 32
+
+FLOPS = 2 * K * H * S + 2 * H * N * S
+
+
+def tile_picked_yimu_cost_p_kernel(
+    tc, x_words, x_scales, w1, w2, accel, dt, lev, vel, posi, tt, wv, wpp, offs, from1, to1, out
+):
+    nc = tc.nc
+    with ExitStack() as ctx:
+        sb = ctx.enter_context(tc.tile_pool(name="sb", bufs=1))
+        ps = ctx.enter_context(tc.psum_pool(name="ps", bufs=1))
+
+        def sbuf(name, shape, dtype):
+            return sb.tile(shape, dtype, name=name, align_bytes=64)
+
+        def bank(name, tag, shape):
+            return ps.tile(shape, F32, name=name, tag=tag)
+
+        offs_sb = sbuf("offs_sb", [P, S // 16], U16)
+        from_sb = sbuf("from_sb", [P, V // 16], U16)
+        to_sb = sbuf("to_sb", [P, V // 16], U16)
+        x_scale_all = sbuf("x_scale_all", [P, T], U8)
+        x_word_all = [sbuf("x_word_all%d" % g, [P, T], I32) for g in range(PASSES)]
+        w1_raw = [sbuf("w1_raw%d" % g, [P, PACK, H], F32) for g in range(PASSES)]
+        w2_raw = sbuf("w2_raw", [P, PACK, N], F32)
+        accel_sb = sbuf("accel_sb", [P, ROW_TILES, S], F32)
+        vel_sb = [sbuf("vel_sb%d" % r, [P, U], F32) for r in range(ROW_TILES)]
+        posi_sb = [sbuf("posi_sb%d" % r, [P, U], F32) for r in range(ROW_TILES)]
+        dt_sb = sbuf("dt_sb", [P, D], F32)
+        lev_sb = sbuf("lev_sb", [P, D], F32)
+        tt_sb = sbuf("tt_sb", [P, V], F32)
+        wv_sb = sbuf("wv_sb", [P, ROW_TILES, 1], F32)
+        wpp_sb = sbuf("wpp_sb", [P, ROW_TILES, 1], F32)
+        ident = sbuf("ident", [P, P], F32)
+
+        def load_w1(g):
+            rows = w1[g * P * PACK:(g + 1) * P * PACK, :]
+            nc.sync.dma_start(out=w1_raw[g][:], in_=rows.rearrange("(p j) c -> p j c", j=PACK))
+
+        def load_scales(q):
+            nc.sync.dma_start(
+                out=x_scale_all[32 * q:32 * q + 4 * PASSES, :].bitcast(I32),
+                in_=x_scales[:, 4 * q:4 * q + 4, :].bitcast(I32),
+            )
+
+        nc.vector.memset(x_scale_all[:].bitcast(I32), 0)
+        make_identity(nc, ident[:])
+        nc.sync.dma_start(out=dt_sb[:], in_=dt[0:1, :].rearrange("o (v d) -> (o v) d", d=D))
+        nc.sync.dma_start(out=lev_sb[:], in_=lev[0:1, :].rearrange("o (v d) -> (o v) d", d=D))
+        load_w1(0)
+        nc.sync.dma_start(from_sb[:], from1)
+        nc.sync.dma_start(to_sb[:], to1)
+        nc.sync.dma_start(out=accel_sb[:], in_=accel.rearrange("(r p) s -> p r s", p=P))
+        load_scales(0)
+        load_scales(1)
+        load_w1(1)
+        load_scales(2)
+        load_scales(3)
+        for r in range(ROW_TILES):
+            nc.sync.dma_start(out=vel_sb[r][:], in_=vel[r * P:(r + 1) * P, :])
+        nc.sync.dma_start(out=tt_sb[:], in_=tt)
+        for r in range(ROW_TILES):
+            nc.sync.dma_start(out=posi_sb[r][:], in_=posi[r * P:(r + 1) * P, :])
+        nc.sync.dma_start(out=w2_raw[:], in_=w2.rearrange("(p j) c -> p j c", j=PACK))
+        nc.sync.dma_start(offs_sb[:], offs)
+        for g in range(PASSES):
+            nc.sync.dma_start(out=x_word_all[g][:], in_=x_words[g].rearrange("p n t -> p (n t)").bitcast(I32))
+        with nc.allow_non_contiguous_dma(reason="one weight a partition"):
+            nc.sync.dma_start(out=wv_sb[:], in_=wv.rearrange("(r p) o -> p r o", p=P))
+            nc.sync.dma_start(out=wpp_sb[:], in_=wpp.rearrange("(r p) o -> p r o", p=P))
+
+        step = [dt_sb, lev_sb]
+        step_gain = [sbuf("step_gain%d" % e, [P, D], F32) for e in range(2)]
+        for e in range(2):
+            nc.scalar.activation(out=step_gain[e][:], in_=step[e][:], func=ACT.Copy, scale=GAIN)
+
+        w1_codes = [sbuf("w1_codes%d" % g, [P, H], U32) for g in range(PASSES)]
+        w1_scale = [sbuf("w1_scale%d" % g, [P, H], U8) for g in range(PASSES)]
+
+        def quantise_w1(g):
+            grouped = sbuf("w1_grouped%d" % g, [P, PACK, P, PACK], BF16)
+            dst = grouped[:].rearrange("p t m j -> p m t j")
+            src = w1_raw[g][:].rearrange("p j (m t) -> p m t j", t=PACK)
+            nc.vector.tensor_copy(out=dst[:, :W1_VECTOR_SHARE], in_=src[:, :W1_VECTOR_SHARE])
+            nc.scalar.copy(out=dst[:, W1_VECTOR_SHARE:], in_=src[:, W1_VECTOR_SHARE:])
+            nc.vector.quantize_mx(
+                out=w1_codes[g][:].bitcast(FP8X4),
+                scales=w1_scale[g][:],
+                in_=grouped[:].rearrange("p t m j -> p (t m j)"),
+            )
+
+        quantise_w1(0)
+
+        accel_t = [bank("accel_t%d" % d, "work%d" % d, [P, N]) for d in range(D)]
+        for d in range(D):
+            for r in range(ROW_TILES):
+                cols = accel_sb[:, r, :].rearrange("p (v d) -> p d v", d=D)[:, d, :]
+                nc.tensor.transpose(accel_t[d][:, r * P:(r + 1) * P], cols, ident[:])
+        base = [[sbuf("base%d_%d" % (e, d), [P, N], F32) for d in range(D + 1)] for e in range(2)]
+        for e in range(2):
+            nc.scalar.activation(out=base[e][0][:], in_=accel_t[0][:], func=ACT.Copy, scale=step[e][:, 0:1])
+        for d in range(1, D):
+            for e in range(2):
+                nc.vector.scalar_tensor_tensor(
+                    base[e][d][:], accel_t[d][:], step[e][:, d:d + 1], base[e][d - 1][:], ALU.mult, ALU.add
+                )
+
+        quantise_w1(1)
+
+        vel_from = sbuf("vel_from", [P, ROW_TILES, V], F32)
+        drift = sbuf("drift", [P, ROW_TILES, V], F32)
+        start = sbuf("start", [P, ROW_TILES, V], F32)
+        moved = [sbuf("moved%d" % e, [P, ROW_TILES, V], F32) for e in range(2)]
+        for r in range(ROW_TILES):
+            nc.scalar.activation(out=vel_from[:, r, :], in_=vel_sb[r][:].indirect(from_sb[:]), func=ACT.Copy)
+        for r in range(ROW_TILES):
+            nc.vector.tensor_tensor(moved[0][:, r, :], vel_sb[r][:].indirect(to_sb[:]), vel_from[:, r, :], ALU.subtract)
+        for r in range(ROW_TILES):
+            nc.vector.tensor_tensor(drift[:, r, :], vel_from[:, r, :], tt_sb[:], ALU.mult)
+        for r in range(ROW_TILES):
+            nc.vector.tensor_tensor(start[:, r, :], posi_sb[r][:].indirect(from_sb[:]), drift[:, r, :], ALU.add)
+        for r in range(ROW_TILES):
+            nc.vector.tensor_tensor(moved[1][:, r, :], posi_sb[r][:].indirect(to_sb[:]), start[:, r, :], ALU.subtract)
+        for e in range(2):
+            moved_t = bank("moved_t%d" % e, "res%d" % (2 * e), [P, N])
+            for r in range(ROW_TILES):
+                nc.tensor.transpose(moved_t[:, r * P:(r + 1) * P], moved[e][:, r, :], ident[:])
+            nc.vector.tensor_tensor(base[e][D][:], base[e][D - 1][:], moved_t[:], ALU.subtract)
+
+        resid = [[bank("resid%d_%d" % (e, r), "res%d" % (2 * e + r), [P, V]) for r in range(ROW_TILES)] for e in range(2)]
+
+        def add_turned(e, term, first, last):
+            for r in range(ROW_TILES):
+                nc.tensor.matmul(resid[e][r][:], term[:, r * P:(r + 1) * P], ident[:], start=first, stop=last, is_transpose=True)
+
+        for e in range(2):
+            add_turned(e, base[e][D], True, False)
+
+        w2_grouped = sbuf("w2_grouped", [P, N, PACK], BF16)
+        w2_codes = sbuf("w2_codes", [P, N], U32)
+        w2_scale = sbuf("w2_scale", [P, N], U8)
+        nc.scalar.copy(
+            out=w2_grouped[:].rearrange("p (c i) j -> p c j i", i=4),
+            in_=w2_raw[:].rearrange("p j (c i) -> p c j i", i=4),
+        )
+        nc.vector.quantize_mx(
+            out=w2_codes[:].bitcast(FP8X4), scales=w2_scale[:], in_=w2_grouped[:].rearrange("p c j -> p (c j)")
+        )
+
+        x_scale = sbuf("x_scale", [P, S], U8)
+        nc.vector.tensor_copy(x_scale[:], x_scale_all[:].indirect(offs_sb[:]))
+        hidden = [bank("hidden%d" % c, "work%d" % c, [P, PACK, CHUNK]) for c in range(CHUNKS)]
+        for g in range(PASSES):
+            for c in range(CHUNKS):
+                x_word = sbuf("x_word%d_%d" % (g, c), [P, CHUNK], U32)
+                picks = offs_sb[:, c * CHUNK // 16:(c + 1) * CHUNK // 16]
+                nc.vector.tensor_copy(x_word[:], x_word_all[g][:].bitcast(U32).indirect(picks))
+                for t in range(PACK):
+                    nc.tensor.matmul_mx(
+                        out=hidden[c][:, t, :],
+                        lhsT=w1_codes[g][:, t * P:(t + 1) * P].bitcast(FP8X4),
+                        lhsT_scale=w1_scale[g][:, t * P:(t + 1) * P],
+                        rhs=x_word[:].bitcast(FP8X4),
+                        rhs_scale=x_scale[4 * g:P, c * CHUNK:(c + 1) * CHUNK],
+                        start=(g == 0 and t == 0),
+                        stop=(g == PASSES - 1 and t == PACK - 1),
+                    )
+
+        h_grouped = sbuf("h_grouped", [P, D, V, PACK], BF16)
+        per_chunk = CHUNK // D
+        for c in range(CHUNKS):
+            dst = h_grouped[:, :, c * per_chunk:(c + 1) * per_chunk, :]
+            src = hidden[c][:].rearrange("p t (v d) -> p d v t", d=D)
+            if c == 2:
+                nc.vector.tensor_scalar(dst, src, 0.0, None, ALU.max)
+            else:
+                nc.scalar.activation(out=dst, in_=src, func=ACT.Relu)
+
+        scaled = [[sbuf("scaled%d_%d" % (e, d), [P, N], F32) for d in range(D)] for e in range(2)]
+        corr = []
+        for d in range(D):
+            h_codes = sbuf("h_codes%d" % d, [P, V], U32)
+            h_scale = sbuf("h_scale%d" % d, [P, V], U8)
+            nc.vector.quantize_mx(
+                out=h_codes[:].bitcast(FP8X4), scales=h_scale[:], in_=h_grouped[:, d].rearrange("p v t -> p (v t)")
+            )
+            corr_d = bank("corr%d" % d, "work%d" % d, [P, N])
+            nc.tensor.matmul_mx(
+                out=corr_d[:],
+                lhsT=h_codes[:].bitcast(FP8X4),
+                lhsT_scale=h_scale[:],
+                rhs=w2_codes[:].bitcast(FP8X4),
+                rhs_scale=w2_scale[:],
+                start=True,
+                stop=True,
+            )
+            corr.append(corr_d)
+        for d in range(D):
+            for e in range(2):
+                factor = step_gain[e][:, d:d + 1]
+                if d % 2 == 0:
+                    nc.scalar.activation(out=scaled[e][d][:], in_=corr[d][:], func=ACT.Copy, scale=factor)
+                else:
+                    nc.vector.scalar_tensor_tensor(
+                        scaled[e][d][:], corr[d][:], factor, scaled[e][d - 1][:], ALU.mult, ALU.add
+                    )
+            if d % 2 == 1:
+                for e in range(2):
+                    add_turned(e, scaled[e][d], False, d == D - 1)
+
+        weight = [wv_sb, wpp_sb]
+        square = [[sbuf("square%d_%d" % (e, r), [P, V], F32) for r in range(ROW_TILES)] for e in range(2)]
+        for e in range(2):
+            for r in range(ROW_TILES):
+                nc.scalar.activation(out=square[e][r][:], in_=resid[e][r][:], func=ACT.Square)
+        part = [sbuf("part%d" % r, [P, V], F32) for r in range(ROW_TILES)]
+        for r in range(ROW_TILES):
+            nc.vector.tensor_scalar(part[r][:], square[0][r][:], weight[0][:, r, :], None, ALU.mult)
+        for r in range(ROW_TILES):
+            cost = sbuf("cost%d" % r, [P, V], F32)
+            nc.vector.scalar_tensor_tensor(cost[:], square[1][r][:], weight[1][:, r, :], part[r][:], ALU.mult, ALU.add)
+            nc.sync.dma_start(out=out[r * P:(r + 1) * P, :], in_=cost[:])

@@ -21,7 +21,6 @@ CHUNK = 128
 CHUNKS = S // CHUNK
 ROW_TILES = N // P
 GAIN = 0.3
-W1_VECTOR_SHARE = 32
 
 FLOPS = 2 * K * H * S + 2 * H * N * S
 
@@ -72,23 +71,21 @@ def tile_picked_yimu_cost_p_kernel(
         nc.sync.dma_start(out=dt_sb[:], in_=dt[0:1, :].rearrange("o (v d) -> (o v) d", d=D))
         nc.sync.dma_start(out=lev_sb[:], in_=lev[0:1, :].rearrange("o (v d) -> (o v) d", d=D))
         load_w1(0)
+        nc.sync.dma_start(out=accel_sb[:], in_=accel.rearrange("(r p) s -> p r s", p=P))
+        for q in range(4):
+            load_scales(q)
+        nc.sync.dma_start(offs_sb[:], offs)
+        load_w1(1)
         nc.sync.dma_start(from_sb[:], from1)
         nc.sync.dma_start(to_sb[:], to1)
-        nc.sync.dma_start(out=accel_sb[:], in_=accel.rearrange("(r p) s -> p r s", p=P))
-        load_scales(0)
-        load_scales(1)
-        load_w1(1)
-        load_scales(2)
-        load_scales(3)
-        for r in range(ROW_TILES):
-            nc.sync.dma_start(out=vel_sb[r][:], in_=vel[r * P:(r + 1) * P, :])
-        nc.sync.dma_start(out=tt_sb[:], in_=tt)
-        for r in range(ROW_TILES):
-            nc.sync.dma_start(out=posi_sb[r][:], in_=posi[r * P:(r + 1) * P, :])
         nc.sync.dma_start(out=w2_raw[:], in_=w2.rearrange("(p j) c -> p j c", j=PACK))
-        nc.sync.dma_start(offs_sb[:], offs)
+        nc.sync.dma_start(out=tt_sb[:], in_=tt)
         for g in range(PASSES):
             nc.sync.dma_start(out=x_word_all[g][:], in_=x_words[g].rearrange("p n t -> p (n t)").bitcast(I32))
+        for r in range(ROW_TILES):
+            nc.sync.dma_start(out=vel_sb[r][:], in_=vel[r * P:(r + 1) * P, :])
+        for r in range(ROW_TILES):
+            nc.sync.dma_start(out=posi_sb[r][:], in_=posi[r * P:(r + 1) * P, :])
         with nc.allow_non_contiguous_dma(reason="one weight a partition"):
             nc.sync.dma_start(out=wv_sb[:], in_=wv.rearrange("(r p) o -> p r o", p=P))
             nc.sync.dma_start(out=wpp_sb[:], in_=wpp.rearrange("(r p) o -> p r o", p=P))
@@ -105,8 +102,7 @@ def tile_picked_yimu_cost_p_kernel(
             grouped = sbuf("w1_grouped%d" % g, [P, PACK, P, PACK], BF16)
             dst = grouped[:].rearrange("p t m j -> p m t j")
             src = w1_raw[g][:].rearrange("p j (m t) -> p m t j", t=PACK)
-            nc.vector.tensor_copy(out=dst[:, :W1_VECTOR_SHARE], in_=src[:, :W1_VECTOR_SHARE])
-            nc.scalar.copy(out=dst[:, W1_VECTOR_SHARE:], in_=src[:, W1_VECTOR_SHARE:])
+            nc.vector.tensor_copy(out=dst, in_=src)
             nc.vector.quantize_mx(
                 out=w1_codes[g][:].bitcast(FP8X4),
                 scales=w1_scale[g][:],
@@ -120,45 +116,24 @@ def tile_picked_yimu_cost_p_kernel(
             for r in range(ROW_TILES):
                 cols = accel_sb[:, r, :].rearrange("p (v d) -> p d v", d=D)[:, d, :]
                 nc.tensor.transpose(accel_t[d][:, r * P:(r + 1) * P], cols, ident[:])
-        base = [[sbuf("base%d_%d" % (e, d), [P, N], F32) for d in range(D + 1)] for e in range(2)]
-        for e in range(2):
-            nc.scalar.activation(out=base[e][0][:], in_=accel_t[0][:], func=ACT.Copy, scale=step[e][:, 0:1])
-        for d in range(1, D):
-            for e in range(2):
-                nc.vector.scalar_tensor_tensor(
-                    base[e][d][:], accel_t[d][:], step[e][:, d:d + 1], base[e][d - 1][:], ALU.mult, ALU.add
-                )
-
-        quantise_w1(1)
-
-        vel_from = sbuf("vel_from", [P, ROW_TILES, V], F32)
-        drift = sbuf("drift", [P, ROW_TILES, V], F32)
-        start = sbuf("start", [P, ROW_TILES, V], F32)
-        moved = [sbuf("moved%d" % e, [P, ROW_TILES, V], F32) for e in range(2)]
-        for r in range(ROW_TILES):
-            nc.scalar.activation(out=vel_from[:, r, :], in_=vel_sb[r][:].indirect(from_sb[:]), func=ACT.Copy)
-        for r in range(ROW_TILES):
-            nc.vector.tensor_tensor(moved[0][:, r, :], vel_sb[r][:].indirect(to_sb[:]), vel_from[:, r, :], ALU.subtract)
-        for r in range(ROW_TILES):
-            nc.vector.tensor_tensor(drift[:, r, :], vel_from[:, r, :], tt_sb[:], ALU.mult)
-        for r in range(ROW_TILES):
-            nc.vector.tensor_tensor(start[:, r, :], posi_sb[r][:].indirect(from_sb[:]), drift[:, r, :], ALU.add)
-        for r in range(ROW_TILES):
-            nc.vector.tensor_tensor(moved[1][:, r, :], posi_sb[r][:].indirect(to_sb[:]), start[:, r, :], ALU.subtract)
-        for e in range(2):
-            moved_t = bank("moved_t%d" % e, "res%d" % (2 * e), [P, N])
-            for r in range(ROW_TILES):
-                nc.tensor.transpose(moved_t[:, r * P:(r + 1) * P], moved[e][:, r, :], ident[:])
-            nc.vector.tensor_tensor(base[e][D][:], base[e][D - 1][:], moved_t[:], ALU.subtract)
-
-        resid = [[bank("resid%d_%d" % (e, r), "res%d" % (2 * e + r), [P, V]) for r in range(ROW_TILES)] for e in range(2)]
+        resid = [bank("resid%d" % e, "res%d" % e, [P, ROW_TILES, V]) for e in range(2)]
 
         def add_turned(e, term, first, last):
             for r in range(ROW_TILES):
-                nc.tensor.matmul(resid[e][r][:], term[:, r * P:(r + 1) * P], ident[:], start=first, stop=last, is_transpose=True)
+                nc.tensor.matmul(
+                    resid[e][:, r, :], term[:, r * P:(r + 1) * P], ident[:],
+                    start=(first and r == 0), stop=(last and r == ROW_TILES - 1), is_transpose=True,
+                )
 
-        for e in range(2):
-            add_turned(e, base[e][D], True, False)
+        for d in range(D):
+            for e in range(2):
+                raw_term = sbuf("raw_term%d_%d" % (e, d), [P, N], F32)
+                nc.scalar.activation(out=raw_term[:], in_=accel_t[d][:], func=ACT.Copy, scale=step[e][:, d:d + 1])
+                add_turned(e, raw_term, d == 0, False)
+
+        x_scale = sbuf("x_scale", [P, S], U8)
+        nc.vector.tensor_copy(x_scale[:], x_scale_all[:].indirect(offs_sb[:]))
+        quantise_w1(1)
 
         w2_grouped = sbuf("w2_grouped", [P, N, PACK], BF16)
         w2_codes = sbuf("w2_codes", [P, N], U32)
@@ -171,8 +146,6 @@ def tile_picked_yimu_cost_p_kernel(
             out=w2_codes[:].bitcast(FP8X4), scales=w2_scale[:], in_=w2_grouped[:].rearrange("p c j -> p (c j)")
         )
 
-        x_scale = sbuf("x_scale", [P, S], U8)
-        nc.vector.tensor_copy(x_scale[:], x_scale_all[:].indirect(offs_sb[:]))
         hidden = [bank("hidden%d" % c, "work%d" % c, [P, PACK, CHUNK]) for c in range(CHUNKS)]
         for g in range(PASSES):
             for c in range(CHUNKS):
@@ -195,10 +168,35 @@ def tile_picked_yimu_cost_p_kernel(
         for c in range(CHUNKS):
             dst = h_grouped[:, :, c * per_chunk:(c + 1) * per_chunk, :]
             src = hidden[c][:].rearrange("p t (v d) -> p d v t", d=D)
-            if c == 2:
+            if c > 0:
                 nc.vector.tensor_scalar(dst, src, 0.0, None, ALU.max)
             else:
                 nc.scalar.activation(out=dst, in_=src, func=ACT.Relu)
+
+        def look_up(picked, table, picks, sign):
+            nc.scalar.activation(out=picked, in_=table[:].indirect(picks[:]), func=ACT.Copy, scale=sign)
+
+        vel_from, vel_to, drift, posi_from, posi_to = [
+            sbuf(name, [P, ROW_TILES, V], F32) for name in ("vel_from", "vel_to", "drift", "posi_from", "posi_to")
+        ]
+        for r in range(ROW_TILES):
+            look_up(vel_from[:, r, :], vel_sb[r], from_sb, 1.0)
+            look_up(vel_to[:, r, :], vel_sb[r], to_sb, -1.0)
+            nc.gpsimd.tensor_tensor(drift[:, r, :], vel_from[:, r, :], tt_sb[:], ALU.mult)
+        for r in range(ROW_TILES):
+            look_up(posi_from[:, r, :], posi_sb[r], from_sb, 1.0)
+            look_up(posi_to[:, r, :], posi_sb[r], to_sb, -1.0)
+        pose_sum = [sbuf("pose_sum%d" % e, [P, N], F32) for e in range(2)]
+        pose_terms = [[vel_from, vel_to], [drift, posi_from, posi_to]]
+        for e in range(2):
+            pose_t = bank("pose_t%d" % e, "pose%d" % e, [P, N])
+            for r in range(ROW_TILES):
+                for i, term in enumerate(pose_terms[e]):
+                    nc.tensor.matmul(
+                        pose_t[:, r * P:(r + 1) * P], term[:, r, :], ident[:],
+                        start=(i == 0), stop=(i == len(pose_terms[e]) - 1), is_transpose=True,
+                    )
+            nc.scalar.copy(out=pose_sum[e][:], in_=pose_t[:])
 
         scaled = [[sbuf("scaled%d_%d" % (e, d), [P, N], F32) for d in range(D)] for e in range(2)]
         corr = []
@@ -219,28 +217,30 @@ def tile_picked_yimu_cost_p_kernel(
                 stop=True,
             )
             corr.append(corr_d)
-        for d in range(D):
+        for e in range(2):
+            nc.vector.tensor_scalar(scaled[e][0][:], corr[0][:], step_gain[e][:, 0:1], None, ALU.mult)
+        for e in range(2):
+            nc.scalar.activation(out=scaled[e][2][:], in_=corr[2][:], func=ACT.Copy, scale=step_gain[e][:, 2:3])
+        for d, before in ((1, 0), (3, 1)):
             for e in range(2):
-                factor = step_gain[e][:, d:d + 1]
-                if d % 2 == 0:
-                    nc.scalar.activation(out=scaled[e][d][:], in_=corr[d][:], func=ACT.Copy, scale=factor)
-                else:
-                    nc.vector.scalar_tensor_tensor(
-                        scaled[e][d][:], corr[d][:], factor, scaled[e][d - 1][:], ALU.mult, ALU.add
-                    )
-            if d % 2 == 1:
-                for e in range(2):
-                    add_turned(e, scaled[e][d], False, d == D - 1)
+                nc.vector.scalar_tensor_tensor(
+                    scaled[e][d][:], corr[d][:], step_gain[e][:, d:d + 1], scaled[e][before][:], ALU.mult, ALU.add
+                )
+        for e in range(2):
+            add_turned(e, scaled[e][2], False, False)
+        for e in range(2):
+            add_turned(e, pose_sum[e], False, False)
+        for e in range(2):
+            add_turned(e, scaled[e][3], False, True)
 
         weight = [wv_sb, wpp_sb]
-        square = [[sbuf("square%d_%d" % (e, r), [P, V], F32) for r in range(ROW_TILES)] for e in range(2)]
+        square = [sbuf("square%d" % e, [P, ROW_TILES, V], F32) for e in range(2)]
         for e in range(2):
-            for r in range(ROW_TILES):
-                nc.scalar.activation(out=square[e][r][:], in_=resid[e][r][:], func=ACT.Square)
+            nc.scalar.activation(out=square[e][:], in_=resid[e][:], func=ACT.Square)
         part = [sbuf("part%d" % r, [P, V], F32) for r in range(ROW_TILES)]
         for r in range(ROW_TILES):
-            nc.vector.tensor_scalar(part[r][:], square[0][r][:], weight[0][:, r, :], None, ALU.mult)
+            nc.vector.tensor_scalar(part[r][:], square[0][:, r, :], weight[0][:, r, :], None, ALU.mult)
         for r in range(ROW_TILES):
             cost = sbuf("cost%d" % r, [P, V], F32)
-            nc.vector.scalar_tensor_tensor(cost[:], square[1][r][:], weight[1][:, r, :], part[r][:], ALU.mult, ALU.add)
+            nc.vector.scalar_tensor_tensor(cost[:], square[1][:, r, :], weight[1][:, r, :], part[r][:], ALU.mult, ALU.add)
             nc.sync.dma_start(out=out[r * P:(r + 1) * P, :], in_=cost[:])

@@ -68,14 +68,14 @@ def tile_picked_yimu_cost_p_kernel(
 
         nc.vector.memset(x_scale_all[:].bitcast(I32), 0)
         make_identity(nc, ident[:])
+        load_w1(0)
         nc.sync.dma_start(out=dt_sb[:], in_=dt[0:1, :].rearrange("o (v d) -> (o v) d", d=D))
         nc.sync.dma_start(out=lev_sb[:], in_=lev[0:1, :].rearrange("o (v d) -> (o v) d", d=D))
-        load_w1(0)
         nc.sync.dma_start(out=accel_sb[:], in_=accel.rearrange("(r p) s -> p r s", p=P))
         for q in range(4):
             load_scales(q)
-        nc.sync.dma_start(offs_sb[:], offs)
         load_w1(1)
+        nc.sync.dma_start(offs_sb[:], offs)
         nc.sync.dma_start(from_sb[:], from1)
         nc.sync.dma_start(to_sb[:], to1)
         nc.sync.dma_start(out=w2_raw[:], in_=w2.rearrange("(p j) c -> p j c", j=PACK))
@@ -100,9 +100,12 @@ def tile_picked_yimu_cost_p_kernel(
 
         def quantise_w1(g):
             grouped = sbuf("w1_grouped%d" % g, [P, PACK, P, PACK], BF16)
-            dst = grouped[:].rearrange("p t m j -> p m t j")
-            src = w1_raw[g][:].rearrange("p j (m t) -> p m t j", t=PACK)
-            nc.vector.tensor_copy(out=dst, in_=src)
+            src = w1_raw[g][:].rearrange("p j (m t) -> p t m j", t=PACK)
+            last = PACK - 1
+            nc.vector.tensor_copy(
+                out=grouped[:, :last].rearrange("p t m j -> p m t j"), in_=src[:, :last].rearrange("p t m j -> p m t j")
+            )
+            nc.scalar.copy(out=grouped[:, last], in_=src[:, last])
             nc.vector.quantize_mx(
                 out=w1_codes[g][:].bitcast(FP8X4),
                 scales=w1_scale[g][:],
@@ -116,14 +119,16 @@ def tile_picked_yimu_cost_p_kernel(
             for r in range(ROW_TILES):
                 cols = accel_sb[:, r, :].rearrange("p (v d) -> p d v", d=D)[:, d, :]
                 nc.tensor.transpose(accel_t[d][:, r * P:(r + 1) * P], cols, ident[:])
-        resid = [bank("resid%d" % e, "res%d" % e, [P, ROW_TILES, V]) for e in range(2)]
+        resid_vel = bank("resid_vel", "resid_vel", [P, ROW_TILES, V])
+        resid_pos = [bank("resid_pos%d" % r, "resid_pos%d" % r, [P, V]) for r in range(ROW_TILES)]
 
         def add_turned(e, term, first, last):
             for r in range(ROW_TILES):
-                nc.tensor.matmul(
-                    resid[e][:, r, :], term[:, r * P:(r + 1) * P], ident[:],
-                    start=(first and r == 0), stop=(last and r == ROW_TILES - 1), is_transpose=True,
-                )
+                if e == 0:
+                    target, opens, closes = resid_vel[:, r, :], first and r == 0, last and r == ROW_TILES - 1
+                else:
+                    target, opens, closes = resid_pos[r][:], first, last
+                nc.tensor.matmul(target, term[:, r * P:(r + 1) * P], ident[:], start=opens, stop=closes, is_transpose=True)
 
         for d in range(D):
             for e in range(2):
@@ -131,9 +136,9 @@ def tile_picked_yimu_cost_p_kernel(
                 nc.scalar.activation(out=raw_term[:], in_=accel_t[d][:], func=ACT.Copy, scale=step[e][:, d:d + 1])
                 add_turned(e, raw_term, d == 0, False)
 
+        quantise_w1(1)
         x_scale = sbuf("x_scale", [P, S], U8)
         nc.vector.tensor_copy(x_scale[:], x_scale_all[:].indirect(offs_sb[:]))
-        quantise_w1(1)
 
         w2_grouped = sbuf("w2_grouped", [P, N, PACK], BF16)
         w2_codes = sbuf("w2_codes", [P, N], U32)
@@ -163,6 +168,19 @@ def tile_picked_yimu_cost_p_kernel(
                         stop=(g == PASSES - 1 and t == PACK - 1),
                     )
 
+        def look_up(picked, table, picks, sign):
+            nc.scalar.activation(out=picked, in_=table[:].indirect(picks[:]), func=ACT.Copy, scale=sign)
+
+        vel_from, vel_to, drift, posi_from, posi_to = [
+            sbuf(name, [P, ROW_TILES, V], F32) for name in ("vel_from", "vel_to", "drift", "posi_from", "posi_to")
+        ]
+        for r in range(ROW_TILES):
+            look_up(vel_from[:, r, :], vel_sb[r], from_sb, 1.0)
+            look_up(vel_to[:, r, :], vel_sb[r], to_sb, -1.0)
+        for r in range(ROW_TILES):
+            look_up(posi_from[:, r, :], posi_sb[r], from_sb, 1.0)
+            look_up(posi_to[:, r, :], posi_sb[r], to_sb, -1.0)
+
         h_grouped = sbuf("h_grouped", [P, D, V, PACK], BF16)
         per_chunk = CHUNK // D
         for c in range(CHUNKS):
@@ -173,30 +191,21 @@ def tile_picked_yimu_cost_p_kernel(
             else:
                 nc.scalar.activation(out=dst, in_=src, func=ACT.Relu)
 
-        def look_up(picked, table, picks, sign):
-            nc.scalar.activation(out=picked, in_=table[:].indirect(picks[:]), func=ACT.Copy, scale=sign)
+        for r in range(ROW_TILES):
+            nc.vector.tensor_tensor(drift[:, r, :], vel_from[:, r, :], tt_sb[:], ALU.mult)
+        pose_sum = sbuf("pose_sum", [P, 2 * N], F32)
 
-        vel_from, vel_to, drift, posi_from, posi_to = [
-            sbuf(name, [P, ROW_TILES, V], F32) for name in ("vel_from", "vel_to", "drift", "posi_from", "posi_to")
-        ]
+        def turn_sum(target, terms, r):
+            for i, term in enumerate(terms):
+                nc.tensor.matmul(
+                    target, term[:, r, :], ident[:], start=(i == 0), stop=(i == len(terms) - 1), is_transpose=True
+                )
+
+        pose_early = bank("pose_early", "pose", [P, 3, P])
         for r in range(ROW_TILES):
-            look_up(vel_from[:, r, :], vel_sb[r], from_sb, 1.0)
-            look_up(vel_to[:, r, :], vel_sb[r], to_sb, -1.0)
-            nc.gpsimd.tensor_tensor(drift[:, r, :], vel_from[:, r, :], tt_sb[:], ALU.mult)
-        for r in range(ROW_TILES):
-            look_up(posi_from[:, r, :], posi_sb[r], from_sb, 1.0)
-            look_up(posi_to[:, r, :], posi_sb[r], to_sb, -1.0)
-        pose_sum = [sbuf("pose_sum%d" % e, [P, N], F32) for e in range(2)]
-        pose_terms = [[vel_from, vel_to], [drift, posi_from, posi_to]]
-        for e in range(2):
-            pose_t = bank("pose_t%d" % e, "pose%d" % e, [P, N])
-            for r in range(ROW_TILES):
-                for i, term in enumerate(pose_terms[e]):
-                    nc.tensor.matmul(
-                        pose_t[:, r * P:(r + 1) * P], term[:, r, :], ident[:],
-                        start=(i == 0), stop=(i == len(pose_terms[e]) - 1), is_transpose=True,
-                    )
-            nc.scalar.copy(out=pose_sum[e][:], in_=pose_t[:])
+            turn_sum(pose_early[:, r, :], [vel_from, vel_to], r)
+        turn_sum(pose_early[:, 2, :], [drift, posi_from, posi_to], 0)
+        nc.scalar.copy(out=pose_sum[:, :3 * P], in_=pose_early[:].rearrange("p a m -> p (a m)"))
 
         scaled = [[sbuf("scaled%d_%d" % (e, d), [P, N], F32) for d in range(D)] for e in range(2)]
         corr = []
@@ -219,8 +228,11 @@ def tile_picked_yimu_cost_p_kernel(
             corr.append(corr_d)
         for e in range(2):
             nc.vector.tensor_scalar(scaled[e][0][:], corr[0][:], step_gain[e][:, 0:1], None, ALU.mult)
+        pose_late = bank("pose_late", "work0", [P, P])
+        turn_sum(pose_late[:], [drift, posi_from, posi_to], 1)
         for e in range(2):
             nc.scalar.activation(out=scaled[e][2][:], in_=corr[2][:], func=ACT.Copy, scale=step_gain[e][:, 2:3])
+        nc.scalar.copy(out=pose_sum[:, 3 * P:], in_=pose_late[:])
         for d, before in ((1, 0), (3, 1)):
             for e in range(2):
                 nc.vector.scalar_tensor_tensor(
@@ -229,14 +241,15 @@ def tile_picked_yimu_cost_p_kernel(
         for e in range(2):
             add_turned(e, scaled[e][2], False, False)
         for e in range(2):
-            add_turned(e, pose_sum[e], False, False)
+            add_turned(e, pose_sum[:, e * N:(e + 1) * N], False, False)
         for e in range(2):
             add_turned(e, scaled[e][3], False, True)
 
         weight = [wv_sb, wpp_sb]
         square = [sbuf("square%d" % e, [P, ROW_TILES, V], F32) for e in range(2)]
-        for e in range(2):
-            nc.scalar.activation(out=square[e][:], in_=resid[e][:], func=ACT.Square)
+        nc.scalar.activation(out=square[0][:], in_=resid_vel[:], func=ACT.Square)
+        for r in range(ROW_TILES):
+            nc.scalar.activation(out=square[1][:, r, :], in_=resid_pos[r][:], func=ACT.Square)
         part = [sbuf("part%d" % r, [P, V], F32) for r in range(ROW_TILES)]
         for r in range(ROW_TILES):
             nc.vector.tensor_scalar(part[r][:], square[0][:, r, :], weight[0][:, r, :], None, ALU.mult)

from contextlib import ExitStack

import concourse.mybir as mybir
from concourse.masks import make_identity

F32 = mybir.dt.float32
BF16 = mybir.dt.bfloat16
I32 = mybir.dt.int32
U32 = mybir.dt.uint32
U16 = mybir.dt.uint16
U8 = mybir.dt.uint8
FP8X4 = mybir.dt.float8_e4m3fn_x4
ALU = mybir.AluOpType
ACT = mybir.ActivationFunctionType

K, T, S, D, H, N, V, U = 1024, 2048, 512, 4, 512, 256, 128, 512
P = 128
PACK = 4
PASSES = K // (P * PACK)
CHUNK = 128
CHUNKS = S // CHUNK
ROW_TILES = N // P
GAIN = 0.3

FLOPS = 2 * K * H * S + 2 * H * N * S


def tile_picked_yimu_cost_p_kernel(
    tc, x_words, x_scales, w1, w2, accel, dt, lev, vel, posi, tt, wv, wpp, offs, from1, to1, out
):
    nc = tc.nc
    with ExitStack() as ctx:
        sb = ctx.enter_context(tc.tile_pool(name="sb", bufs=1))
        ps = ctx.enter_context(tc.psum_pool(name="ps", bufs=1))

        def sbuf(name, shape, dtype):
            return sb.tile(shape, dtype, name=name, align_bytes=64)

        def bank(name, tag, shape):
            return ps.tile(shape, F32, name=name, tag=tag)

        offs_sb = sbuf("offs_sb", [P, S // 16], U16)
        from_sb = sbuf("from_sb", [P, V // 16], U16)
        to_sb = sbuf("to_sb", [P, V // 16], U16)
        x_scale_all = sbuf("x_scale_all", [P, T], U8)
        x_word_all = [sbuf("x_word_all%d" % g, [P, T], I32) for g in range(PASSES)]
        w1_raw = [sbuf("w1_raw%d" % g, [P, PACK, H], F32) for g in range(PASSES)]
        w2_raw = sbuf("w2_raw", [P, PACK, N], F32)
        accel_sb = sbuf("accel_sb", [P, ROW_TILES, S], F32)
        vel_sb = [sbuf("vel_sb%d" % r, [P, U], F32) for r in range(ROW_TILES)]
        posi_sb = [sbuf("posi_sb%d" % r, [P, U], F32) for r in range(ROW_TILES)]
        dt_sb = sbuf("dt_sb", [P, D], F32)
        lev_sb = sbuf("lev_sb", [P, D], F32)
        tt_sb = sbuf("tt_sb", [P, V], F32)
        wv_sb = sbuf("wv_sb", [P, ROW_TILES, 1], F32)
        wpp_sb = sbuf("wpp_sb", [P, ROW_TILES, 1], F32)
        ident = sbuf("ident", [P, P], F32)

        def load_w1(g):
            rows = w1[g * P * PACK:(g + 1) * P * PACK, :]
            nc.sync.dma_start(out=w1_raw[g][:], in_=rows.rearrange("(p j) c -> p j c", j=PACK))

        def load_scales(q):
            nc.sync.dma_start(
                out=x_scale_all[32 * q:32 * q + 4 * PASSES, :].bitcast(I32),
                in_=x_scales[:, 4 * q:4 * q + 4, :].bitcast(I32),
            )

        nc.vector.memset(x_scale_all[:].bitcast(I32), 0)
        make_identity(nc, ident[:])
        load_w1(0)
        nc.sync.dma_start(out=dt_sb[:], in_=dt[0:1, :].rearrange("o (v d) -> (o v) d", d=D))
        nc.sync.dma_start(out=lev_sb[:], in_=lev[0:1, :].rearrange("o (v d) -> (o v) d", d=D))
        nc.sync.dma_start(out=accel_sb[:], in_=accel.rearrange("(r p) s -> p r s", p=P))
        for q in range(4):
            load_scales(q)
        load_w1(1)
        nc.sync.dma_start(offs_sb[:], offs)
        nc.sync.dma_start(from_sb[:], from1)
        nc.sync.dma_start(to_sb[:], to1)
        nc.sync.dma_start(out=w2_raw[:], in_=w2.rearrange("(p j) c -> p j c", j=PACK))
        nc.sync.dma_start(out=tt_sb[:], in_=tt)
        for g in range(PASSES):
            nc.sync.dma_start(out=x_word_all[g][:], in_=x_words[g].rearrange("p n t -> p (n t)").bitcast(I32))
        for r in range(ROW_TILES):
            nc.sync.dma_start(out=vel_sb[r][:], in_=vel[r * P:(r + 1) * P, :])
        for r in range(ROW_TILES):
            nc.sync.dma_start(out=posi_sb[r][:], in_=posi[r * P:(r + 1) * P, :])
        with nc.allow_non_contiguous_dma(reason="one weight a partition"):
            nc.sync.dma_start(out=wv_sb[:], in_=wv.rearrange("(r p) o -> p r o", p=P))
            nc.sync.dma_start(out=wpp_sb[:], in_=wpp.rearrange("(r p) o -> p r o", p=P))

        step = [dt_sb, lev_sb]
        step_gain = [sbuf("step_gain%d" % e, [P, D], F32) for e in range(2)]
        for e in range(2):
            nc.scalar.activation(out=step_gain[e][:], in_=step[e][:], func=ACT.Copy, scale=GAIN)

        w1_codes = [sbuf("w1_codes%d" % g, [P, H], U32) for g in range(PASSES)]
        w1_scale = [sbuf("w1_scale%d" % g, [P, H], U8) for g in range(PASSES)]

        def quantise_w1(g):
            grouped = sbuf("w1_grouped%d" % g, [P, PACK, P, PACK], BF16)
            src = w1_raw[g][:].rearrange("p j (m t) -> p t m j", t=PACK)
            last = PACK - 1
            nc.vector.tensor_copy(
                out=grouped[:, :last].rearrange("p t m j -> p m t j"), in_=src[:, :last].rearrange("p t m j -> p m t j")
            )
            nc.scalar.copy(out=grouped[:, last], in_=src[:, last])
            nc.vector.quantize_mx(
                out=w1_codes[g][:].bitcast(FP8X4),
                scales=w1_scale[g][:],
                in_=grouped[:].rearrange("p t m j -> p (t m j)"),
            )

        quantise_w1(0)

        accel_t = [bank("accel_t%d" % d, "work%d" % d, [P, N]) for d in range(D)]
        for d in range(D):
            for r in range(ROW_TILES):
                cols = accel_sb[:, r, :].rearrange("p (v d) -> p d v", d=D)[:, d, :]
                nc.tensor.transpose(accel_t[d][:, r * P:(r + 1) * P], cols, ident[:])
        resid_vel = bank("resid_vel", "resid_vel", [P, ROW_TILES, V])
        resid_pos = [bank("resid_pos%d" % r, "resid_pos%d" % r, [P, V]) for r in range(ROW_TILES)]

        def add_turned(e, term, first, last):
            for r in range(ROW_TILES):
                if e == 0:
                    target, opens, closes = resid_vel[:, r, :], first and r == 0, last and r == ROW_TILES - 1
                else:
                    target, opens, closes = resid_pos[r][:], first, last
                nc.tensor.matmul(target, term[:, r * P:(r + 1) * P], ident[:], start=opens, stop=closes, is_transpose=True)

        for d in range(D):
            for e in range(2):
                raw_term = sbuf("raw_term%d_%d" % (e, d), [P, N], F32)
                nc.scalar.activation(out=raw_term[:], in_=accel_t[d][:], func=ACT.Copy, scale=step[e][:, d:d + 1])
                add_turned(e, raw_term, d == 0, False)

        quantise_w1(1)
        x_scale = sbuf("x_scale", [P, S], U8)
        nc.vector.tensor_copy(x_scale[:], x_scale_all[:].indirect(offs_sb[:]))

        w2_grouped = sbuf("w2_grouped", [P, N, PACK], BF16)
        w2_codes = sbuf("w2_codes", [P, N], U32)
        w2_scale = sbuf("w2_scale", [P, N], U8)
        nc.scalar.copy(
            out=w2_grouped[:].rearrange("p (c i) j -> p c j i", i=4),
            in_=w2_raw[:].rearrange("p j (c i) -> p c j i", i=4),
        )
        nc.vector.quantize_mx(
            out=w2_codes[:].bitcast(FP8X4), scales=w2_scale[:], in_=w2_grouped[:].rearrange("p c j -> p (c j)")
        )

        hidden = [bank("hidden%d" % c, "work%d" % c, [P, PACK, CHUNK]) for c in range(CHUNKS)]
        for g in range(PASSES):
            for c in range(CHUNKS):
                x_word = sbuf("x_word%d_%d" % (g, c), [P, CHUNK], U32)
                picks = offs_sb[:, c * CHUNK // 16:(c + 1) * CHUNK // 16]
                nc.vector.tensor_copy(x_word[:], x_word_all[g][:].bitcast(U32).indirect(picks))
                for t in range(PACK):
                    nc.tensor.matmul_mx(
                        out=hidden[c][:, t, :],
                        lhsT=w1_codes[g][:, t * P:(t + 1) * P].bitcast(FP8X4),
                        lhsT_scale=w1_scale[g][:, t * P:(t + 1) * P],
                        rhs=x_word[:].bitcast(FP8X4),
                        rhs_scale=x_scale[4 * g:P, c * CHUNK:(c + 1) * CHUNK],
                        start=(g == 0 and t == 0),
                        stop=(g == PASSES - 1 and t == PACK - 1),
                    )

        def look_up(picked, table, picks, sign):
            nc.scalar.activation(out=picked, in_=table[:].indirect(picks[:]), func=ACT.Copy, scale=sign)

        vel_from, vel_to, drift, posi_from, posi_to = [
            sbuf(name, [P, ROW_TILES, V], F32) for name in ("vel_from", "vel_to", "drift", "posi_from", "posi_to")
        ]
        for r in range(ROW_TILES):
            look_up(vel_from[:, r, :], vel_sb[r], from_sb, 1.0)
            look_up(vel_to[:, r, :], vel_sb[r], to_sb, -1.0)
        for r in range(ROW_TILES):
            look_up(posi_from[:, r, :], posi_sb[r], from_sb, 1.0)
            look_up(posi_to[:, r, :], posi_sb[r], to_sb, -1.0)

        h_grouped = sbuf("h_grouped", [P, D, V, PACK], BF16)
        per_chunk = CHUNK // D
        for c in range(CHUNKS):
            dst = h_grouped[:, :, c * per_chunk:(c + 1) * per_chunk, :]
            src = hidden[c][:].rearrange("p t (v d) -> p d v t", d=D)
            if c > 0:
                nc.vector.tensor_scalar(dst, src, 0.0, None, ALU.max)
            else:
                nc.scalar.activation(out=dst, in_=src, func=ACT.Relu)

        for r in range(ROW_TILES):
            nc.vector.tensor_tensor(drift[:, r, :], vel_from[:, r, :], tt_sb[:], ALU.mult)
        pose_sum = sbuf("pose_sum", [P, 2 * N], F32)

        def turn_sum(target, terms, r):
            for i, term in enumerate(terms):
                nc.tensor.matmul(
                    target, term[:, r, :], ident[:], start=(i == 0), stop=(i == len(terms) - 1), is_transpose=True
                )

        pose_early = bank("pose_early", "pose", [P, 3, P])
        for r in range(ROW_TILES):
            turn_sum(pose_early[:, r, :], [vel_from, vel_to], r)
        turn_sum(pose_early[:, 2, :], [drift, posi_from, posi_to], 0)
        nc.scalar.copy(out=pose_sum[:, :3 * P], in_=pose_early[:].rearrange("p a m -> p (a m)"))

        scaled = [[sbuf("scaled%d_%d" % (e, d), [P, N], F32) for d in range(D)] for e in range(2)]
        corr = []
        for d in range(D):
            h_codes = sbuf("h_codes%d" % d, [P, V], U32)
            h_scale = sbuf("h_scale%d" % d, [P, V], U8)
            nc.vector.quantize_mx(
                out=h_codes[:].bitcast(FP8X4), scales=h_scale[:], in_=h_grouped[:, d].rearrange("p v t -> p (v t)")
            )
            corr_d = bank("corr%d" % d, "work%d" % d, [P, N])
            nc.tensor.matmul_mx(
                out=corr_d[:],
                lhsT=h_codes[:].bitcast(FP8X4),
                lhsT_scale=h_scale[:],
                rhs=w2_codes[:].bitcast(FP8X4),
                rhs_scale=w2_scale[:],
                start=True,
                stop=True,
            )
            corr.append(corr_d)
        for e in range(2):
            nc.vector.tensor_scalar(scaled[e][0][:], corr[0][:], step_gain[e][:, 0:1], None, ALU.mult)
        pose_late = bank("pose_late", "work0", [P, P])
        turn_sum(pose_late[:], [drift, posi_from, posi_to], 1)
        for e in range(2):
            nc.scalar.activation(out=scaled[e][2][:], in_=corr[2][:], func=ACT.Copy, scale=step_gain[e][:, 2:3])
        nc.scalar.copy(out=pose_sum[:, 3 * P:], in_=pose_late[:])
        for d, before in ((1, 0), (3, 1)):
            for e in range(2):
                nc.vector.scalar_tensor_tensor(
                    scaled[e][d][:], corr[d][:], step_gain[e][:, d:d + 1], scaled[e][before][:], ALU.mult, ALU.add
                )
        for e in range(2):
            add_turned(e, scaled[e][2], False, False)
        for e in range(2):
            add_turned(e, pose_sum[:, e * N:(e + 1) * N], False, False)
        for e in range(2):
            add_turned(e, scaled[e][3], False, True)

        weight = [wv_sb, wpp_sb]
        square = [sbuf("square%d" % e, [P, ROW_TILES, V], F32) for e in range(2)]
        nc.scalar.activation(out=square[0][:], in_=resid_vel[:], func=ACT.Square)
        for r in range(ROW_TILES):
            nc.scalar.activation(out=square[1][:, r, :], in_=resid_pos[r][:], func=ACT.Square)
        part = [sbuf("part%d" % r, [P, V], F32) for r in range(ROW_TILES)]
        for r in range(ROW_TILES):
            nc.vector.tensor_scalar(part[r][:], square[0][:, r, :], weight[0][:, r, :], None, ALU.mult)
        for r in range(ROW_TILES):
            cost = sbuf("cost%d" % r, [P, V], F32)
            nc.vector.scalar_tensor_tensor(cost[:], square[1][:, r, :], weight[1][:, r, :], part[r][:], ALU.mult, ALU.add)
            nc.sync.dma_start(out=out[r * P:(r + 1) * P, :], in_=cost[:])
